import numpy as np
import ml_dtypes


def mxq(x, axis, fmt="e4m3"):
    dtype, down = {"e4m3": (ml_dtypes.float8_e4m3fn, 7), "e5m2": (ml_dtypes.float8_e5m2, 14)}[fmt]
    v = np.moveaxis(np.asarray(x, np.float32).astype(ml_dtypes.bfloat16).astype(np.float64), axis, -1)
    blocks = v.reshape(v.shape[:-1] + (-1, 32))
    amax = np.abs(blocks).max(-1, keepdims=True)
    byte = np.maximum(np.where(amax > 0, np.frexp(amax)[1] - 1 + 127, 0) - down, 1)
    scale = np.exp2(byte - 127.0)
    codes = (blocks / scale).astype(np.float32).astype(dtype).astype(np.float64)
    return np.moveaxis((codes * scale).reshape(v.shape), -1, axis)


WIDE = False


def mx_kscale(k):
    if not WIDE:
        return np.ones(k)
    levels = np.array([10, -10, 5, -5, 0])
    if k % 512:
        return np.exp2(np.random.permutation(np.resize(levels, k // 32))).repeat(32)
    a = np.empty((k // 512, 16))
    for p in range(k // 512):
        a[p, :8] = np.random.permutation(np.resize(levels, 8))
        for g in range(8):
            far = levels[np.abs(levels - a[p, g]) >= 10]
            a[p, g + 8] = far[np.random.randint(len(far))]
    return np.exp2(a.ravel()).repeat(32)


BF16 = ml_dtypes.bfloat16


def bf(x):
    return np.asarray(x, np.float32).astype(BF16)


def f64(x):
    return np.asarray(x).astype(np.float64)


E2M1 = np.array([0.0, 0.5, 1.0, 1.5, 2.0, 3.0, 4.0, 6.0, -0.0, -0.5, -1.0, -1.5, -2.0, -3.0, -4.0, -6.0])


def pack_weight(w, fmt):
    k, n = w.shape
    w = f64(bf(w)).reshape(k // 32, 32, n)
    amax = np.abs(w).max(1)
    if fmt == "e4m3":
        byte = np.frexp(amax)[1] - 1 + 127 - 7
    else:
        mant, ex = np.frexp(amax / 6.0)
        byte = np.where(mant > 0.5, ex, ex - 1) + 127
    byte = np.clip(np.where(amax > 0, byte, 1), 1, 254)
    scaled = (w * np.exp2(127.0 - byte)[:, None, :]).reshape(k, n).astype(np.float32)
    by_word = np.ascontiguousarray(scaled.reshape(k // 512, 128, 4, n).transpose(0, 1, 3, 2))
    if fmt == "e4m3":
        words = by_word.astype(ml_dtypes.float8_e4m3fn).view(np.uint8)
    else:
        c = by_word.astype(ml_dtypes.float4_e2m1fn).view(np.uint8) & 0xF
        words = c[..., 0::2] | (c[..., 1::2] << 4)
    return np.ascontiguousarray(words), np.ascontiguousarray(byte.astype(np.uint8).reshape(k // 512, 16, n))


def unpack_weight(words, scales, fmt):
    g, p, n, _ = words.shape
    if fmt == "e4m3":
        vals = np.ascontiguousarray(words).view(ml_dtypes.float8_e4m3fn).astype(np.float64)
    else:
        nib = np.empty((g, p, n, 4), np.uint8)
        nib[..., 0::2] = words & 0xF
        nib[..., 1::2] = words >> 4
        vals = E2M1[nib]
    vals = vals * np.repeat(np.exp2(scales.astype(np.float64) - 127.0), 8, axis=1)[..., None]
    return vals.transpose(0, 1, 3, 2).reshape(g * 512, n)
def pack4(w):
    words, scales = pack_weight(w, "e2m1")
    return words.reshape(words.shape[0], 128, -1), scales


def unpack4(words, scales):
    return unpack_weight(words.reshape(words.shape[0], 128, -1, 2), scales, "e2m1")


M, F, D, N, R = 1536, 2048, 1024, 512, 256


def draw0():
    s = mx_kscale(F)
    t = mx_kscale(D)
    u = mx_kscale(M)
    gate = np.random.standard_normal((M, F))
    up = np.random.standard_normal((M, F)) * s * u[:, None]
    w_down = np.random.standard_normal((F, D)) / np.sqrt(F) / s[:, None] * t
    resid = np.random.standard_normal((M, D)) * t * u[:, None]
    head_words, head_scales = pack4(np.random.standard_normal((D, N)) / np.sqrt(D) / t[:, None])
    pool = np.random.standard_normal((R, M)) / np.sqrt(M) / u
    return {"gate": bf(gate), "up": bf(up), "w_down": bf(w_down), "resid": bf(resid),
            "head_words": head_words, "head_scales": head_scales, "pool": bf(pool)}


def core(gate, up, w_down, resid, head_words, head_scales, pool):
    h = np.maximum(f64(gate), 0.0) * f64(up)
    z = (mxq(h, 1, "e4m3") @ mxq(f64(w_down), 0, "e4m3")) + f64(resid)
    y = mxq(z, 1, "e4m3") @ unpack4(head_words, head_scales)
    c = mxq(f64(pool), 1, "e4m3") @ mxq(z, 0, "e4m3")
    return y, c


def e4m3fn_bytes(y):
    return np.clip(np.asarray(y, np.float64), -448.0, 448.0).astype(np.float32).astype(ml_dtypes.float8_e4m3fn).view(np.uint8)


def e4m3fn_values(b):
    return np.asarray(b, np.uint8).view(ml_dtypes.float8_e4m3fn).astype(np.float64)


def setup_inputs():
    d = draw0()
    x0 = np.asarray(d['pool']).astype(np.float64)
    s = (np.max(np.abs(x0), axis=(0,), keepdims=True) / 448.0).astype(np.float32)
    out = {}
    for k, v in d.items():
        if k == 'pool':
            out['pool_bytes'] = e4m3fn_bytes(x0 / s.astype(np.float64))
            out['pool_scale'] = s
        else:
            out[k] = v
    return out


def reference(gate, up, w_down, resid, head_words, head_scales, pool_bytes, pool_scale):
    return core(gate, up, w_down, resid, head_words, head_scales, e4m3fn_values(pool_bytes) * pool_scale.astype(np.float64))

@@ -1,0 +1,419 @@
+from contextlib import ExitStack
+
+import concourse.mybir as mybir
+from concourse.masks import make_identity
+
+M, F, D, N, R = 1536, 2048, 1024, 512, 256
+FLOPS = 2 * M * F * D + 2 * M * D * N + 2 * R * M * D
+
+F32 = mybir.dt.float32
+BF16 = mybir.dt.bfloat16
+U32 = mybir.dt.uint32
+U8 = mybir.dt.uint8
+I32 = mybir.dt.int32
+FP8 = mybir.dt.float8_e4m3fn
+FP8X4 = mybir.dt.float8_e4m3fn_x4
+FP4X4 = mybir.dt.float4_e2m1fn_x4
+ADD = mybir.AluOpType.add
+MULT = mybir.AluOpType.mult
+
+P = 128
+PACK = 4
+K_PASS = P * PACK
+TILES = M // P
+GROUPS = M // K_PASS
+F_PASSES = F // K_PASS
+D_PASSES = D // K_PASS
+HALF = 512
+CHUNK = 256
+CHUNKS = D // CHUNK
+BUFS_IN = 4
+
+
+def tile_reglu_down_two_reads_s8_kernel(
+    tc, gate, up, w_down, resid, head_words, head_scales, pool_bytes, pool_scale, out_y, out_c
+):
+    nc = tc.nc
+
+    gate_v = gate.rearrange("(g p t) f -> g p t f", p=P, t=PACK)
+    up_v = up.rearrange("(g p t) f -> g p t f", p=P, t=PACK)
+    resid_v = resid.rearrange("(g p t) d -> g p t d", p=P, t=PACK)
+    y_v = out_y.rearrange("(g p t) n -> g p t n", p=P, t=PACK)
+    w_v = w_down.rearrange("(g p j) d -> g p j d", p=P, j=PACK)
+
+    with ExitStack() as ctx:
+        keep = ctx.enter_context(tc.tile_pool(name="keep", bufs=1))
+        sb = ctx.enter_context(tc.tile_pool(name="sb", bufs=2))
+        psum = ctx.enter_context(tc.psum_pool(name="psum", bufs=1))
+
+        w_codes = keep.tile([P, F_PASSES, D], U32, name="w_codes", align_bytes=64)
+        w_scales = keep.tile([P, F_PASSES, D], U8, name="w_scales", align_bytes=64)
+        z_codes = keep.tile([P, GROUPS, D], U32, name="z_codes", align_bytes=64)
+        z_scales = keep.tile([P, GROUPS, D], U8, name="z_scales", align_bytes=64)
+        pool_codes = keep.tile([P, GROUPS, R], U32, name="pool_codes", align_bytes=64)
+        pool_scales = keep.tile([P, GROUPS, R], U8, name="pool_scales", align_bytes=64)
+        head_sb = keep.tile([P, D_PASSES, 2 * N], U8, name="head_sb", align_bytes=64)
+        head_sc = keep.tile([P, D_PASSES, N], U8, name="head_sc", align_bytes=64)
+        code_bytes = keep.tile([P, R // P, M], U8, name="code_bytes", align_bytes=64)
+        scale_row = keep.tile([P, M], F32, name="scale_row", align_bytes=64)
+        pool_bf = keep.tile([P, R // P, M], BF16, name="pool_bf", align_bytes=64)
+        ident = keep.tile([P, P], F32, name="ident", align_bytes=64)
+        warm = keep.tile([P, 2], F32, name="warm", align_bytes=64)
+
+        gates, ups, resids, relus, hs, hcs, hss = {}, {}, {}, {}, {}, {}, {}
+        hbanks, hts, accs, zs, zbanks, zts, zcs, zss, ybanks = {}, {}, {}, {}, {}, {}, {}, {}, {}
+        wraws, wgs, zis, pbanks, pts, cbanks, couts = {}, {}, {}, {}, {}, {}, {}
+
+        def load_gate(i):
+            if i < TILES:
+                gates[i] = sb.tile([P, F], BF16, tag="gate", name="gate_sb", bufs=BUFS_IN, align_bytes=64)
+                nc.sync.dma_start(out=gates[i][:], in_=gate_v[i // PACK][:, i % PACK, :])
+
+        def load_up(i):
+            if i < TILES:
+                ups[i] = sb.tile([P, F], BF16, tag="up", name="up_sb", bufs=BUFS_IN, align_bytes=64)
+                nc.sync.dma_start(out=ups[i][:], in_=up_v[i // PACK][:, i % PACK, :])
+
+        def load_resid(i):
+            if i < TILES:
+                resids[i] = sb.tile([P, D], BF16, tag="resid", name="resid_sb", bufs=4, align_bytes=64)
+                nc.sync.dma_start(out=resids[i][:], in_=resid_v[i // PACK][:, i % PACK, :])
+
+        def load_w(g, h):
+            wraws[g, h] = sb.tile([P, PACK, HALF], BF16, tag="wraw", name="w_raw", bufs=4, align_bytes=64)
+            nc.sync.dma_start(out=wraws[g, h][:], in_=w_v[g][:, :, h * HALF : (h + 1) * HALF])
+
+        def group_w(engine, g, h, c0, c1):
+            if (g, h) not in wgs:
+                wgs[g, h] = sb.tile([P, HALF, PACK], BF16, tag="wg", name="w_grouped", bufs=3, align_bytes=64)
+            dst = wgs[g, h][:, c0:c1, :]
+            src = wraws[g, h][:, :, c0:c1].rearrange("p j w -> p w j")
+            if engine == "v":
+                nc.vector.tensor_copy(out=dst, in_=src)
+            else:
+                nc.scalar.copy(out=dst, in_=src)
+
+        def quant_w(g, h):
+            cols = slice(h * HALF, (h + 1) * HALF)
+            nc.vector.quantize_mx(
+                out=w_codes[:, g, cols].bitcast(FP8X4),
+                scales=w_scales[:, g, cols],
+                in_=wgs[g, h][:].rearrange("p w j -> p (w j)"),
+            )
+
+        def relu(i):
+            if i < TILES:
+                relus[i] = sb.tile([P, F], BF16, tag="relu", name="relu_sb", bufs=2, align_bytes=64)
+                nc.vector.tensor_scalar_max(relus[i][:], gates[i][:], 0.0)
+
+        def product(i):
+            if i < TILES:
+                hs[i] = sb.tile([P, F], BF16, tag="h", name="h_sb", bufs=2, align_bytes=64)
+                nc.vector.tensor_tensor(
+                    out=hs[i][:].rearrange("p (u q e) -> p u q e", u=2, e=2),
+                    in0=relus[i][:].rearrange("p (q u e) -> p u q e", u=2, e=2),
+                    in1=ups[i][:].rearrange("p (q u e) -> p u q e", u=2, e=2),
+                    op=MULT,
+                )
+
+        def turn_h(i):
+            words = hs[i][:].bitcast(F32)
+            for b in range(2):
+                bank = psum.tile([P, 2, 2, P], F32, tag="th", name="h_turned", bufs=2)
+                hbanks[i, b] = bank
+                for gl in range(2):
+                    for u in range(2):
+                        w0 = u * (F // 4) + (2 * b + gl) * P
+                        nc.tensor.transpose(bank[:, gl, u, :], words[:, w0 : w0 + P], ident[:])
+
+        def empty_h(i, b):
+            if b == 0:
+                hts[i] = sb.tile([P, F_PASSES, P, 2], F32, tag="ht", name="h_grouped", bufs=2, align_bytes=64)
+            nc.scalar.copy(
+                out=hts[i][:, 2 * b : 2 * b + 2, :, :], in_=hbanks[i, b][:].rearrange("p g u m -> p g m u")
+            )
+
+        def quant_h(i):
+            hcs[i] = sb.tile([P, F_PASSES * P], U32, tag="hc", name="h_codes", bufs=2, align_bytes=64)
+            hss[i] = sb.tile([P, F_PASSES * P], U8, tag="hsc", name="h_scales", bufs=2, align_bytes=64)
+            nc.vector.quantize_mx(
+                out=hcs[i][:].bitcast(FP8X4),
+                scales=hss[i][:],
+                in_=hts[i][:].rearrange("p g m u -> p (g m u)").bitcast(BF16),
+            )
+
+        def down(i, h):
+            acc = psum.tile([P, HALF], F32, tag="acc", name="z_acc", bufs=4)
+            accs[i, h] = acc
+            for g in range(F_PASSES):
+                cols = slice(h * HALF, (h + 1) * HALF)
+                toks = slice(g * P, (g + 1) * P)
+                nc.tensor.matmul_mx(
+                    out=acc[:],
+                    lhsT=hcs[i][:, toks].bitcast(FP8X4),
+                    lhsT_scale=hss[i][:, toks],
+                    rhs=w_codes[:, g, cols].bitcast(FP8X4),
+                    rhs_scale=w_scales[:, g, cols],
+                    start=(g == 0),
+                    stop=(g == F_PASSES - 1),
+                )
+
+        def add_resid(i, h):
+            G, t = divmod(i, PACK)
+            if G not in zs:
+                zs[G] = sb.tile([P, PACK, D], BF16, tag="z", name="z_sb", bufs=2, align_bytes=64)
+            cols = slice(h * HALF, (h + 1) * HALF)
+            nc.vector.tensor_tensor(
+                out=zs[G][:, t, cols].rearrange("p (u q e) -> p u q e", u=2, e=2),
+                in0=accs[i, h][:].rearrange("p (q u e) -> p u q e", u=2, e=2),
+                in1=resids[i][:, cols].rearrange("p (q u e) -> p u q e", u=2, e=2),
+                op=ADD,
+            )
+
+        def turn_z(i):
+            G, t = divmod(i, PACK)
+            words = zs[G][:, t, :].bitcast(F32)
+            zbanks[i] = psum.tile([P, D_PASSES, 2, P], F32, tag="m", name="z_turned", bufs=2)
+            for h in range(D_PASSES):
+                for u in range(2):
+                    w0 = h * (HALF // 2) + u * P
+                    nc.tensor.transpose(zbanks[i][:, h, u, :], words[:, w0 : w0 + P], ident[:])
+
+        def empty_z(i):
+            zts[i] = sb.tile([P, D_PASSES, P, 2], F32, tag="zt", name="zt_grouped", bufs=2, align_bytes=64)
+            nc.scalar.copy(out=zts[i][:], in_=zbanks[i][:].rearrange("p h u m -> p h m u"))
+
+        def quant_zt(i):
+            zcs[i] = sb.tile([P, D_PASSES * P], U32, tag="ztc", name="zt_codes", bufs=2, align_bytes=64)
+            zss[i] = sb.tile([P, D_PASSES * P], U8, tag="zts", name="zt_scales", bufs=2, align_bytes=64)
+            nc.vector.quantize_mx(
+                out=zcs[i][:].bitcast(FP8X4),
+                scales=zss[i][:],
+                in_=zts[i][:].rearrange("p h m u -> p (h m u)").bitcast(BF16),
+            )
+
+        def project(i):
+            ybanks[i] = psum.tile([P, N], F32, tag="m", name="y_acc", bufs=2)
+            for h in range(D_PASSES):
+                toks = slice(h * P, (h + 1) * P)
+                nc.tensor.matmul_mx(
+                    out=ybanks[i][:],
+                    lhsT=zcs[i][:, toks].bitcast(FP8X4),
+                    lhsT_scale=zss[i][:, toks],
+                    rhs=head_sb[:, h, :].bitcast(FP4X4),
+                    rhs_scale=head_sc[:, h, :],
+                    start=(h == 0),
+                    stop=(h == D_PASSES - 1),
+                )
+
+        def store_y(i):
+            y = sb.tile([P, N], F32, tag="y", name="y_sb", bufs=3, align_bytes=64)
+            nc.scalar.copy(out=y[:], in_=ybanks[i][:])
+            nc.sync.dma_start(out=y_v[i // PACK][:, i % PACK, :], in_=y[:])
+
+        def group_z(engine, G, c):
+            zis[G, c] = sb.tile([P, CHUNK, PACK], BF16, tag="zi", name="z_grouped", bufs=4, align_bytes=64)
+            src = zs[G][:, :, c * CHUNK : (c + 1) * CHUNK].rearrange("p t d -> p d t")
+            if engine == "v":
+                nc.vector.tensor_copy(out=zis[G, c][:], in_=src)
+            else:
+                nc.scalar.copy(out=zis[G, c][:], in_=src)
+
+        def quant_z(G, c):
+            cols = slice(c * CHUNK, (c + 1) * CHUNK)
+            nc.vector.quantize_mx(
+                out=z_codes[:, G, cols].bitcast(FP8X4),
+                scales=z_scales[:, G, cols],
+                in_=zis[G, c][:].rearrange("p d t -> p (d t)"),
+            )
+
+        def scale_pool(G, a):
+            toks = slice(G * K_PASS, (G + 1) * K_PASS)
+            nc.vector.tensor_tensor(
+                out=pool_bf[:, a, toks], in0=code_bytes[:, a, toks].bitcast(FP8), in1=scale_row[:, toks], op=MULT
+            )
+
+        def turn_pool(G):
+            pbanks[G] = psum.tile([P, R // P, 2, P], F32, tag="m", name="pool_turned", bufs=2)
+            for a in range(R // P):
+                words = pool_bf[:, a, G * K_PASS : (G + 1) * K_PASS].bitcast(F32)
+                for u in range(2):
+                    nc.tensor.transpose(pbanks[G][:, a, u, :], words[:, u : K_PASS // 2 : 2], ident[:])
+
+        def empty_pool(G):
+            pts[G] = sb.tile([P, R // P, P, 2], F32, tag="zt", name="pool_grouped", bufs=2, align_bytes=64)
+            nc.scalar.copy(out=pts[G][:], in_=pbanks[G][:].rearrange("p a u r -> p a r u"))
+
+        def quant_pool(G):
+            nc.vector.quantize_mx(
+                out=pool_codes[:, G, :].bitcast(FP8X4),
+                scales=pool_scales[:, G, :],
+                in_=pts[G][:].rearrange("p a r u -> p (a r u)").bitcast(BF16),
+            )
+
+        def gather(h, groups):
+            for a in range(R // P):
+                if (a, h) not in cbanks:
+                    cbanks[a, h] = psum.tile(
+                        [P, HALF], F32, tag=("th", "acc")[h], name="c_acc", bufs=(2, 4)[h]
+                    )
+                cols = slice(h * HALF, (h + 1) * HALF)
+                slots = slice(a * P, (a + 1) * P)
+                for G in groups:
+                    nc.tensor.matmul_mx(
+                        out=cbanks[a, h][:],
+                        lhsT=pool_codes[:, G, slots].bitcast(FP8X4),
+                        lhsT_scale=pool_scales[:, G, slots],
+                        rhs=z_codes[:, G, cols].bitcast(FP8X4),
+                        rhs_scale=z_scales[:, G, cols],
+                        start=(G == 0),
+                        stop=(G == GROUPS - 1),
+                    )
+
+        def store_c(engine, a, h):
+            c_sb = sb.tile([P, HALF], F32, tag="c", name="c_sb", bufs=4, align_bytes=64)
+            dst = c_sb[:].rearrange("p (q u e) -> p q u e", u=2, e=2)
+            src = cbanks[a, h][:].rearrange("p (u q e) -> p q u e", u=2, e=2)
+            if engine == "v":
+                nc.vector.tensor_copy(out=dst, in_=src)
+            else:
+                nc.scalar.copy(out=dst, in_=src)
+            nc.sync.dma_start(out=out_c[a * P : (a + 1) * P, h * HALF : (h + 1) * HALF], in_=c_sb[:])
+
+        with tc.manual_schedule():
+            nc.vector.memset(head_sc[:].rearrange("p g n -> p (g n)").bitcast(I32), 0)
+            nc.vector.memset(warm[:], 0.0)
+            nc.scalar.copy(out=warm[:, 0:1], in_=warm[:, 1:2])
+            make_identity(nc, ident[:])
+
+            load_gate(0)
+            load_w(0, 0)
+            load_up(0)
+            load_w(0, 1)
+            load_w(1, 0)
+            load_w(1, 1)
+            load_gate(1)
+
+            relu(0)
+            group_w("s", 0, 0, 0, HALF)
+            product(0)
+            turn_h(0)
+            group_w("v", 0, 1, 0, HALF)
+            load_w(2, 0)
+            load_up(1)
+            load_w(2, 1)
+            empty_h(0, 0)
+            empty_h(0, 1)
+            quant_w(0, 0)
+            group_w("s", 1, 0, 0, HALF)
+            load_w(3, 0)
+            quant_w(0, 1)
+            group_w("v", 1, 1, 0, HALF)
+            load_w(3, 1)
+            load_resid(0)
+            for q in range(4):
+                rows = slice(32 * q, 32 * q + 4)
+                nc.sync.dma_start(
+                    out=head_sc[rows, :, :].bitcast(I32),
+                    in_=head_scales[:, 4 * q : 4 * q + 4, :].rearrange("g q n -> q g n").bitcast(I32),
+                )
+            load_gate(2)
+            load_up(2)
+            load_resid(1)
+            quant_h(0)
+            relu(1)
+            quant_w(1, 1)
+            quant_w(1, 0)
+            group_w("s", 2, 0, 0, HALF)
+            product(1)
+            relu(2)
+            group_w("v", 2, 1, 0, HALF)
+            quant_w(2, 0)
+            group_w("v", 3, 0, 0, HALF)
+            group_w("s", 3, 1, 0, HALF // 2)
+            quant_w(2, 1)
+            group_w("v", 3, 1, HALF // 2, HALF)
+            quant_w(3, 0)
+            quant_w(3, 1)
+            nc.sync.dma_start(out=head_sb[:], in_=head_words.rearrange("g p b -> p g b"))
+            load_gate(3)
+            load_up(3)
+            load_resid(2)
+            load_gate(4)
+            load_up(4)
+            load_gate(5)
+            load_up(5)
+            load_gate(6)
+
+            for s in range(TILES):
+                if s + 1 < TILES:
+                    turn_h(s + 1)
+                if s in (6, 7, 8):
+                    turn_pool(s - 6)
+                if s >= 1:
+                    turn_z(s - 1)
+                if s >= 2:
+                    store_y(s - 2)
+                product(s + 2)
+                load_up(s + 6)
+                load_resid(s + 3)
+                relu(s + 3)
+                load_gate(s + 7)
+                if s == 0:
+                    nc.sync.dma_start(out=code_bytes[:], in_=pool_bytes.rearrange("(a p) m -> p a m", p=P))
+                    nc.sync.dma_start(
+                        out=scale_row[:], in_=pool_scale.rearrange("o k -> (o k)").partition_broadcast(P)
+                    )
+                if s + 1 < TILES:
+                    empty_h(s + 1, 0)
+                if s >= 1:
+                    empty_z(s - 1)
+                if s + 1 < TILES:
+                    empty_h(s + 1, 1)
+                if s in (6, 7, 8):
+                    empty_pool(s - 6)
+                if s >= 1:
+                    quant_zt(s - 1)
+                if s + 1 < TILES:
+                    quant_h(s + 1)
+                if s in (3, 4, 5):
+                    scale_pool(s - 3, 0)
+                    scale_pool(s - 3, 1)
+                if s in (6, 7, 8):
+                    quant_pool(s - 6)
+                if s >= 5:
+                    quant_z((s - 5) // CHUNKS, (s - 5) % CHUNKS)
+                down(s, 0)
+                down(s, 1)
+                add_resid(s, 0)
+                add_resid(s, 1)
+                if s >= 4:
+                    group_z("s", (s - 4) // CHUNKS, (s - 4) % CHUNKS)
+                if s >= 1:
+                    project(s - 1)
+
+            last = TILES - 1
+            G = GROUPS - 1
+            quant_z(G - 1, CHUNKS - 1)
+            gather(0, range(G))
+            group_z("s", G, 0)
+            group_z("v", G, 1)
+            turn_z(last)
+            store_y(last - 1)
+            group_z("v", G, 2)
+            empty_z(last)
+            quant_z(G, 0)
+            quant_z(G, 1)
+            group_z("s", G, 3)
+            gather(0, range(G, GROUPS))
+            quant_zt(last)
+            project(last)
+            gather(1, range(G))
+            store_c("s", 0, 0)
+            store_c("v", 1, 0)
+            quant_z(G, 2)
+            quant_z(G, 3)
+            gather(1, range(G, GROUPS))
+            store_y(last)
+            store_c("s", 0, 1)
+            store_c("v", 1, 1)

@@ -28,6 +28,9 @@ HALF = 512
 CHUNK = 256
 CHUNKS = D // CHUNK
 BUFS_IN = 4
+RUN = 4
+S_COLS = (256, 256)
+POOL_STEPS = (9, 10, 11)
 
 
 def tile_reglu_down_two_reads_s8_kernel(
@@ -80,18 +83,22 @@ def tile_reglu_down_two_reads_s8_kernel(
                 nc.sync.dma_start(out=resids[i][:], in_=resid_v[i // PACK][:, i % PACK, :])
 
         def load_w(g, h):
-            wraws[g, h] = sb.tile([P, PACK, HALF], BF16, tag="wraw", name="w_raw", bufs=4, align_bytes=64)
+            wraws[g, h] = sb.tile([P, PACK, HALF], BF16, tag="wraw", name="w_raw", bufs=8, align_bytes=64)
             nc.sync.dma_start(out=wraws[g, h][:], in_=w_v[g][:, :, h * HALF : (h + 1) * HALF])
 
         def group_w(engine, g, h, c0, c1):
             if (g, h) not in wgs:
                 wgs[g, h] = sb.tile([P, HALF, PACK], BF16, tag="wg", name="w_grouped", bufs=3, align_bytes=64)
-            dst = wgs[g, h][:, c0:c1, :]
-            src = wraws[g, h][:, :, c0:c1].rearrange("p j w -> p w j")
+            dst = wgs[g, h][:, c0:c1, :].rearrange("p (c i) j -> p c j i", i=RUN)
+            src = wraws[g, h][:, :, c0:c1].rearrange("p j (c i) -> p c j i", i=RUN)
             if engine == "v":
                 nc.vector.tensor_copy(out=dst, in_=src)
             else:
                 nc.scalar.copy(out=dst, in_=src)
+
+        def group_w_split(g, h):
+            group_w("s", g, h, 0, S_COLS[h])
+            group_w("v", g, h, S_COLS[h], HALF)
 
         def quant_w(g, h):
             cols = slice(h * HALF, (h + 1) * HALF)
@@ -211,13 +218,15 @@ def tile_reglu_down_two_reads_s8_kernel(
             nc.scalar.copy(out=y[:], in_=ybanks[i][:])
             nc.sync.dma_start(out=y_v[i // PACK][:, i % PACK, :], in_=y[:])
 
-        def group_z(engine, G, c):
-            zis[G, c] = sb.tile([P, CHUNK, PACK], BF16, tag="zi", name="z_grouped", bufs=4, align_bytes=64)
-            src = zs[G][:, :, c * CHUNK : (c + 1) * CHUNK].rearrange("p t d -> p d t")
+        def group_z(engine, G, c, d0, d1):
+            if (G, c) not in zis:
+                zis[G, c] = sb.tile([P, CHUNK, PACK], BF16, tag="zi", name="z_grouped", bufs=4, align_bytes=64)
+            dst = zis[G, c][:, d0:d1, :].rearrange("p (c i) t -> p c t i", i=RUN)
+            src = zs[G][:, :, c * CHUNK + d0 : c * CHUNK + d1].rearrange("p t (c i) -> p c t i", i=RUN)
             if engine == "v":
-                nc.vector.tensor_copy(out=zis[G, c][:], in_=src)
+                nc.vector.tensor_copy(out=dst, in_=src)
             else:
-                nc.scalar.copy(out=zis[G, c][:], in_=src)
+                nc.scalar.copy(out=dst, in_=src)
 
         def quant_z(G, c):
             cols = slice(c * CHUNK, (c + 1) * CHUNK)
@@ -233,8 +242,8 @@ def tile_reglu_down_two_reads_s8_kernel(
                 out=pool_bf[:, a, toks], in0=code_bytes[:, a, toks].bitcast(FP8), in1=scale_row[:, toks], op=MULT
             )
 
-        def turn_pool(G):
-            pbanks[G] = psum.tile([P, R // P, 2, P], F32, tag="m", name="pool_turned", bufs=2)
+        def turn_pool(G, tag):
+            pbanks[G] = psum.tile([P, R // P, 2, P], F32, tag=tag, name="pool_turned", bufs=2)
             for a in range(R // P):
                 words = pool_bf[:, a, G * K_PASS : (G + 1) * K_PASS].bitcast(F32)
                 for u in range(2):
@@ -289,131 +298,154 @@ def tile_reglu_down_two_reads_s8_kernel(
             load_gate(0)
             load_w(0, 0)
             load_up(0)
-            load_w(0, 1)
             load_w(1, 0)
-            load_w(1, 1)
-            load_gate(1)
-
-            relu(0)
-            group_w("s", 0, 0, 0, HALF)
-            product(0)
-            turn_h(0)
-            group_w("v", 0, 1, 0, HALF)
             load_w(2, 0)
-            load_up(1)
-            load_w(2, 1)
-            empty_h(0, 0)
-            empty_h(0, 1)
-            quant_w(0, 0)
-            group_w("s", 1, 0, 0, HALF)
             load_w(3, 0)
-            quant_w(0, 1)
-            group_w("v", 1, 1, 0, HALF)
-            load_w(3, 1)
+            load_gate(1)
+            load_up(1)
             load_resid(0)
+            load_w(0, 1)
+            load_w(1, 1)
+            load_w(2, 1)
+            load_w(3, 1)
+            load_gate(2)
+            load_up(2)
+            load_resid(1)
             for q in range(4):
                 rows = slice(32 * q, 32 * q + 4)
                 nc.sync.dma_start(
                     out=head_sc[rows, :, :].bitcast(I32),
                     in_=head_scales[:, 4 * q : 4 * q + 4, :].rearrange("g q n -> q g n").bitcast(I32),
                 )
-            load_gate(2)
-            load_up(2)
-            load_resid(1)
-            quant_h(0)
-            relu(1)
-            quant_w(1, 1)
-            quant_w(1, 0)
-            group_w("s", 2, 0, 0, HALF)
-            product(1)
-            relu(2)
-            group_w("v", 2, 1, 0, HALF)
-            quant_w(2, 0)
-            group_w("v", 3, 0, 0, HALF)
-            group_w("s", 3, 1, 0, HALF // 2)
-            quant_w(2, 1)
-            group_w("v", 3, 1, HALF // 2, HALF)
-            quant_w(3, 0)
-            quant_w(3, 1)
             nc.sync.dma_start(out=head_sb[:], in_=head_words.rearrange("g p b -> p g b"))
             load_gate(3)
             load_up(3)
             load_resid(2)
+
+            relu(0)
+            group_w_split(0, 0)
+            product(0)
+            turn_h(0)
+            quant_w(0, 0)
+            group_w_split(1, 0)
+            empty_h(0, 0)
+            empty_h(0, 1)
+            group_w_split(2, 0)
+            quant_w(1, 0)
+            quant_h(0)
+            group_w_split(3, 0)
+            quant_w(2, 0)
+            relu(1)
+            quant_w(3, 0)
+            down(0, 0)
+            product(1)
+            turn_h(1)
+            group_w_split(0, 1)
+            empty_h(1, 0)
+            empty_h(1, 1)
+            group_w_split(1, 1)
+            quant_w(0, 1)
+            add_resid(0, 0)
+            quant_h(1)
+            group_w_split(2, 1)
+            down(1, 0)
+            quant_w(1, 1)
+            group_w_split(3, 1)
+            quant_w(2, 1)
+            relu(2)
+            quant_w(3, 1)
+            down(0, 1)
+            down(1, 1)
+            product(2)
+            add_resid(1, 0)
+            add_resid(0, 1)
             load_gate(4)
             load_up(4)
+            relu(3)
+            add_resid(1, 1)
             load_gate(5)
             load_up(5)
             load_gate(6)
+            load_up(6)
+            load_gate(7)
 
-            for s in range(TILES):
+            for s in range(1, TILES):
                 if s + 1 < TILES:
                     turn_h(s + 1)
-                if s in (6, 7, 8):
-                    turn_pool(s - 6)
-                if s >= 1:
-                    turn_z(s - 1)
+                if s == TILES - 1:
+                    turn_pool(0, "th")
+                    turn_pool(1, "th")
+                turn_z(s - 1)
                 if s >= 2:
                     store_y(s - 2)
                 product(s + 2)
+                load_resid(s + 2)
                 load_up(s + 6)
-                load_resid(s + 3)
                 relu(s + 3)
                 load_gate(s + 7)
-                if s == 0:
+                if s == 4:
                     nc.sync.dma_start(out=code_bytes[:], in_=pool_bytes.rearrange("(a p) m -> p a m", p=P))
-                    nc.sync.dma_start(
-                        out=scale_row[:], in_=pool_scale.rearrange("o k -> (o k)").partition_broadcast(P)
-                    )
+                    nc.sync.dma_start(out=scale_row[:], in_=pool_scale.rearrange("o k -> (o k)").partition_broadcast(P))
                 if s + 1 < TILES:
                     empty_h(s + 1, 0)
-                if s >= 1:
-                    empty_z(s - 1)
+                else:
+                    empty_pool(0)
+                empty_z(s - 1)
                 if s + 1 < TILES:
                     empty_h(s + 1, 1)
-                if s in (6, 7, 8):
-                    empty_pool(s - 6)
-                if s >= 1:
-                    quant_zt(s - 1)
+                else:
+                    empty_pool(1)
+                quant_zt(s - 1)
                 if s + 1 < TILES:
                     quant_h(s + 1)
-                if s in (3, 4, 5):
-                    scale_pool(s - 3, 0)
-                    scale_pool(s - 3, 1)
-                if s in (6, 7, 8):
-                    quant_pool(s - 6)
                 if s >= 5:
                     quant_z((s - 5) // CHUNKS, (s - 5) % CHUNKS)
-                down(s, 0)
-                down(s, 1)
-                add_resid(s, 0)
-                add_resid(s, 1)
+                if s == 9:
+                    scale_pool(0, 0)
+                if s == 10:
+                    scale_pool(0, 1)
+                    scale_pool(1, 0)
+                    scale_pool(1, 1)
+                if s == 11:
+                    quant_pool(0)
+                    quant_pool(1)
+                    scale_pool(2, 0)
+                    scale_pool(2, 1)
+                if s >= 2:
+                    down(s, 0)
+                    down(s, 1)
+                    add_resid(s, 0)
+                    add_resid(s, 1)
                 if s >= 4:
-                    group_z("s", (s - 4) // CHUNKS, (s - 4) % CHUNKS)
-                if s >= 1:
-                    project(s - 1)
+                    group_z("s", (s - 4) // CHUNKS, (s - 4) % CHUNKS, 0, CHUNK)
+                project(s - 1)
 
             last = TILES - 1
             G = GROUPS - 1
+            group_z("s", G, 0, 0, CHUNK)
             quant_z(G - 1, CHUNKS - 1)
+            group_z("v", G, 1, 0, CHUNK)
             gather(0, range(G))
-            group_z("s", G, 0)
-            group_z("v", G, 1)
             turn_z(last)
+            turn_pool(2, "m")
+            gather(1, range(G))
             store_y(last - 1)
-            group_z("v", G, 2)
             empty_z(last)
+            group_z("v", G, 2, 0, CHUNK)
             quant_z(G, 0)
             quant_z(G, 1)
-            group_z("s", G, 3)
-            gather(0, range(G, GROUPS))
+            empty_pool(2)
+            group_z("s", G, 3, 0, CHUNK // 2)
             quant_zt(last)
-            project(last)
-            gather(1, range(G))
-            store_c("s", 0, 0)
-            store_c("v", 1, 0)
+            group_z("v", G, 3, CHUNK // 2, CHUNK)
+            quant_pool(2)
             quant_z(G, 2)
+            project(last)
             quant_z(G, 3)
+            gather(0, range(G, GROUPS))
             gather(1, range(G, GROUPS))
             store_y(last)
-            store_c("s", 0, 1)
-            store_c("v", 1, 1)
+            store_c("v", 0, 0)
+            store_c("s", 1, 0)
+            store_c("v", 0, 1)
+            store_c("s", 1, 1)

@@ -8,14 +8,15 @@ FLOPS = 2 * M * F * D + 2 * M * D * N + 2 * R * M * D
 
 F32 = mybir.dt.float32
 BF16 = mybir.dt.bfloat16
+I32 = mybir.dt.int32
 U32 = mybir.dt.uint32
 U8 = mybir.dt.uint8
-I32 = mybir.dt.int32
 FP8 = mybir.dt.float8_e4m3fn
 FP8X4 = mybir.dt.float8_e4m3fn_x4
 FP4X4 = mybir.dt.float4_e2m1fn_x4
 ADD = mybir.AluOpType.add
 MULT = mybir.AluOpType.mult
+RELU = mybir.ActivationFunctionType.Relu
 
 P = 128
 PACK = 4
@@ -23,14 +24,16 @@ K_PASS = P * PACK
 TILES = M // P
 GROUPS = M // K_PASS
 F_PASSES = F // K_PASS
-D_PASSES = D // K_PASS
 HALF = 512
-CHUNK = 256
-CHUNKS = D // CHUNK
-BUFS_IN = 4
+HALVES = D // HALF
+CHUNK = HALF // 2
+SLOT_TILES = R // P
+
+W_SPLIT = HALF // 2
+ALL = slice(0, F)
+LEFT, RIGHT = slice(0, F // 2), slice(F // 2, F)
+RELU_VECTOR, RELU_SCALAR = slice(0, 7 * F // 8), slice(7 * F // 8, F)
 RUN = 4
-S_COLS = (256, 256)
-POOL_STEPS = (9, 10, 11)
 
 
 def tile_reglu_down_two_reads_s8_kernel(
@@ -47,7 +50,7 @@ def tile_reglu_down_two_reads_s8_kernel(
     with ExitStack() as ctx:
         keep = ctx.enter_context(tc.tile_pool(name="keep", bufs=1))
         sb = ctx.enter_context(tc.tile_pool(name="sb", bufs=2))
-        psum = ctx.enter_context(tc.psum_pool(name="psum", bufs=1))
+        psum = ctx.enter_context(tc.psum_pool(name="psum", bufs=2))
 
         w_codes = keep.tile([P, F_PASSES, D], U32, name="w_codes", align_bytes=64)
         w_scales = keep.tile([P, F_PASSES, D], U8, name="w_scales", align_bytes=64)
@@ -55,27 +58,29 @@ def tile_reglu_down_two_reads_s8_kernel(
         z_scales = keep.tile([P, GROUPS, D], U8, name="z_scales", align_bytes=64)
         pool_codes = keep.tile([P, GROUPS, R], U32, name="pool_codes", align_bytes=64)
         pool_scales = keep.tile([P, GROUPS, R], U8, name="pool_scales", align_bytes=64)
-        head_sb = keep.tile([P, D_PASSES, 2 * N], U8, name="head_sb", align_bytes=64)
-        head_sc = keep.tile([P, D_PASSES, N], U8, name="head_sc", align_bytes=64)
-        code_bytes = keep.tile([P, R // P, M], U8, name="code_bytes", align_bytes=64)
+        head_sb = keep.tile([P, HALVES, 2 * N], U8, name="head_sb", align_bytes=64)
+        head_sc = keep.tile([P, HALVES, N], U8, name="head_sc", align_bytes=64)
+        code_bytes = keep.tile([P, SLOT_TILES, M], U8, name="code_bytes", align_bytes=64)
         scale_row = keep.tile([P, M], F32, name="scale_row", align_bytes=64)
-        pool_bf = keep.tile([P, R // P, M], BF16, name="pool_bf", align_bytes=64)
+        pool_bf = keep.tile([P, SLOT_TILES, M], BF16, name="pool_bf", align_bytes=64)
         ident = keep.tile([P, P], F32, name="ident", align_bytes=64)
-        warm = keep.tile([P, 2], F32, name="warm", align_bytes=64)
 
-        gates, ups, resids, relus, hs, hcs, hss = {}, {}, {}, {}, {}, {}, {}
-        hbanks, hts, accs, zs, zbanks, zts, zcs, zss, ybanks = {}, {}, {}, {}, {}, {}, {}, {}, {}
-        wraws, wgs, zis, pbanks, pts, cbanks, couts = {}, {}, {}, {}, {}, {}, {}
+        gates, ups, resids, relus, hs, hbanks, hts, hcs, hss = {}, {}, {}, {}, {}, {}, {}, {}, {}
+        accs, zs, zbanks, zts, zcs, zss, ybanks = {}, {}, {}, {}, {}, {}, {}
+        wraws, wgs, zis, pbanks, pts, cbanks = {}, {}, {}, {}, {}, {}
 
-        def load_gate(i):
+
+        def load_gate(i, cols=ALL):
             if i < TILES:
-                gates[i] = sb.tile([P, F], BF16, tag="gate", name="gate_sb", bufs=BUFS_IN, align_bytes=64)
-                nc.sync.dma_start(out=gates[i][:], in_=gate_v[i // PACK][:, i % PACK, :])
+                if i not in gates:
+                    gates[i] = sb.tile([P, F], BF16, tag="gate", name="gate_sb", bufs=4, align_bytes=64)
+                nc.sync.dma_start(out=gates[i][:, cols], in_=gate_v[i // PACK][:, i % PACK, cols])
 
-        def load_up(i):
+        def load_up(i, cols=ALL):
             if i < TILES:
-                ups[i] = sb.tile([P, F], BF16, tag="up", name="up_sb", bufs=BUFS_IN, align_bytes=64)
-                nc.sync.dma_start(out=ups[i][:], in_=up_v[i // PACK][:, i % PACK, :])
+                if i not in ups:
+                    ups[i] = sb.tile([P, F], BF16, tag="up", name="up_sb", bufs=4, align_bytes=64)
+                nc.sync.dma_start(out=ups[i][:, cols], in_=up_v[i // PACK][:, i % PACK, cols])
 
         def load_resid(i):
             if i < TILES:
@@ -86,19 +91,29 @@ def tile_reglu_down_two_reads_s8_kernel(
             wraws[g, h] = sb.tile([P, PACK, HALF], BF16, tag="wraw", name="w_raw", bufs=8, align_bytes=64)
             nc.sync.dma_start(out=wraws[g, h][:], in_=w_v[g][:, :, h * HALF : (h + 1) * HALF])
 
-        def group_w(engine, g, h, c0, c1):
-            if (g, h) not in wgs:
-                wgs[g, h] = sb.tile([P, HALF, PACK], BF16, tag="wg", name="w_grouped", bufs=3, align_bytes=64)
-            dst = wgs[g, h][:, c0:c1, :].rearrange("p (c i) j -> p c j i", i=RUN)
-            src = wraws[g, h][:, :, c0:c1].rearrange("p j (c i) -> p c j i", i=RUN)
-            if engine == "v":
-                nc.vector.tensor_copy(out=dst, in_=src)
-            else:
-                nc.scalar.copy(out=dst, in_=src)
+        def load_head():
+            nc.sync.dma_start(out=head_sb[:], in_=head_words.rearrange("g p b -> p g b"))
 
-        def group_w_split(g, h):
-            group_w("s", g, h, 0, S_COLS[h])
-            group_w("v", g, h, S_COLS[h], HALF)
+        def load_head_scales():
+            for q in range(PACK):
+                rows = slice(32 * q, 32 * q + 4)
+                nc.sync.dma_start(
+                    out=head_sc[rows, :, :].bitcast(I32),
+                    in_=head_scales[:, 4 * q : 4 * q + 4, :].rearrange("g q n -> q g n").bitcast(I32),
+                )
+
+        def load_pool():
+            nc.sync.dma_start(out=scale_row[:], in_=pool_scale.rearrange("o k -> (o k)").partition_broadcast(P))
+            nc.sync.dma_start(out=code_bytes[:], in_=pool_bytes.rearrange("(a p) m -> p a m", p=P))
+
+
+        def group_w(g, h):
+            wgs[g, h] = sb.tile([P, HALF, PACK], BF16, tag="wg", name="w_grouped", bufs=3, align_bytes=64)
+            for copy, cols in ((nc.scalar.copy, slice(0, W_SPLIT)), (nc.vector.tensor_copy, slice(W_SPLIT, HALF))):
+                copy(
+                    out=wgs[g, h][:, cols, :].rearrange("p (c i) j -> p c j i", i=RUN),
+                    in_=wraws[g, h][:, :, cols].rearrange("p j (c i) -> p c j i", i=RUN),
+                )
 
         def quant_w(g, h):
             cols = slice(h * HALF, (h + 1) * HALF)
@@ -108,33 +123,43 @@ def tile_reglu_down_two_reads_s8_kernel(
                 in_=wgs[g, h][:].rearrange("p w j -> p (w j)"),
             )
 
-        def relu(i):
-            if i < TILES:
-                relus[i] = sb.tile([P, F], BF16, tag="relu", name="relu_sb", bufs=2, align_bytes=64)
-                nc.vector.tensor_scalar_max(relus[i][:], gates[i][:], 0.0)
 
-        def product(i):
+        def relu_tile(i):
+            if i not in relus:
+                relus[i] = sb.tile([P, F], BF16, tag="relu", name="relu_sb", bufs=2, align_bytes=64)
+            return relus[i]
+
+        def relu_v(i, cols):
             if i < TILES:
-                hs[i] = sb.tile([P, F], BF16, tag="h", name="h_sb", bufs=2, align_bytes=64)
+                nc.vector.tensor_scalar_max(relu_tile(i)[:, cols], gates[i][:, cols], 0.0)
+
+        def relu_s(i, cols):
+            if i < TILES:
+                nc.scalar.activation(relu_tile(i)[:, cols], gates[i][:, cols], func=RELU)
+
+        def product(i, cols=ALL):
+            if i < TILES:
+                if i not in hs:
+                    hs[i] = sb.tile([P, F], BF16, tag="h", name="h_sb", bufs=2, align_bytes=64)
+                quads = slice(cols.start // 4, cols.stop // 4)
                 nc.vector.tensor_tensor(
-                    out=hs[i][:].rearrange("p (u q e) -> p u q e", u=2, e=2),
-                    in0=relus[i][:].rearrange("p (q u e) -> p u q e", u=2, e=2),
-                    in1=ups[i][:].rearrange("p (q u e) -> p u q e", u=2, e=2),
+                    out=hs[i][:].rearrange("p (u q e) -> p u q e", u=2, e=2)[:, :, quads, :],
+                    in0=relus[i][:, cols].rearrange("p (q u e) -> p u q e", u=2, e=2),
+                    in1=ups[i][:, cols].rearrange("p (q u e) -> p u q e", u=2, e=2),
                     op=MULT,
                 )
 
         def turn_h(i):
             words = hs[i][:].bitcast(F32)
             for b in range(2):
-                bank = psum.tile([P, 2, 2, P], F32, tag="th", name="h_turned", bufs=2)
-                hbanks[i, b] = bank
-                for gl in range(2):
+                hbanks[i, b] = psum.tile([P, 2, 2, P], F32, tag="turned", name="h_turned", bufs=2)
+                for gb in range(2):
                     for u in range(2):
-                        w0 = u * (F // 4) + (2 * b + gl) * P
-                        nc.tensor.transpose(bank[:, gl, u, :], words[:, w0 : w0 + P], ident[:])
+                        w0 = u * (F // 4) + (2 * b + gb) * P
+                        nc.tensor.transpose(hbanks[i, b][:, gb, u, :], words[:, w0 : w0 + P], ident[:])
 
         def empty_h(i, b):
-            if b == 0:
+            if i not in hts:
                 hts[i] = sb.tile([P, F_PASSES, P, 2], F32, tag="ht", name="h_grouped", bufs=2, align_bytes=64)
             nc.scalar.copy(
                 out=hts[i][:, 2 * b : 2 * b + 2, :, :], in_=hbanks[i, b][:].rearrange("p g u m -> p g m u")
@@ -142,21 +167,21 @@ def tile_reglu_down_two_reads_s8_kernel(
 
         def quant_h(i):
             hcs[i] = sb.tile([P, F_PASSES * P], U32, tag="hc", name="h_codes", bufs=2, align_bytes=64)
-            hss[i] = sb.tile([P, F_PASSES * P], U8, tag="hsc", name="h_scales", bufs=2, align_bytes=64)
+            hss[i] = sb.tile([P, F_PASSES * P], U8, tag="hs", name="h_scales", bufs=2, align_bytes=64)
             nc.vector.quantize_mx(
                 out=hcs[i][:].bitcast(FP8X4),
                 scales=hss[i][:],
                 in_=hts[i][:].rearrange("p g m u -> p (g m u)").bitcast(BF16),
             )
 
+
         def down(i, h):
-            acc = psum.tile([P, HALF], F32, tag="acc", name="z_acc", bufs=4)
-            accs[i, h] = acc
+            accs[i, h] = psum.tile([P, HALF], F32, tag="acc", name="z_acc", bufs=4)
+            cols = slice(h * HALF, (h + 1) * HALF)
             for g in range(F_PASSES):
-                cols = slice(h * HALF, (h + 1) * HALF)
                 toks = slice(g * P, (g + 1) * P)
                 nc.tensor.matmul_mx(
-                    out=acc[:],
+                    out=accs[i, h][:],
                     lhsT=hcs[i][:, toks].bitcast(FP8X4),
                     lhsT_scale=hss[i][:, toks],
                     rhs=w_codes[:, g, cols].bitcast(FP8X4),
@@ -177,22 +202,23 @@ def tile_reglu_down_two_reads_s8_kernel(
                 op=ADD,
             )
 
+
         def turn_z(i):
             G, t = divmod(i, PACK)
             words = zs[G][:, t, :].bitcast(F32)
-            zbanks[i] = psum.tile([P, D_PASSES, 2, P], F32, tag="m", name="z_turned", bufs=2)
-            for h in range(D_PASSES):
+            zbanks[i] = psum.tile([P, HALVES, 2, P], F32, tag="mixed", name="z_turned", bufs=2)
+            for h in range(HALVES):
                 for u in range(2):
                     w0 = h * (HALF // 2) + u * P
                     nc.tensor.transpose(zbanks[i][:, h, u, :], words[:, w0 : w0 + P], ident[:])
 
         def empty_z(i):
-            zts[i] = sb.tile([P, D_PASSES, P, 2], F32, tag="zt", name="zt_grouped", bufs=2, align_bytes=64)
+            zts[i] = sb.tile([P, HALVES, P, 2], F32, tag="zt", name="zt_grouped", bufs=2, align_bytes=64)
             nc.scalar.copy(out=zts[i][:], in_=zbanks[i][:].rearrange("p h u m -> p h m u"))
 
         def quant_zt(i):
-            zcs[i] = sb.tile([P, D_PASSES * P], U32, tag="ztc", name="zt_codes", bufs=2, align_bytes=64)
-            zss[i] = sb.tile([P, D_PASSES * P], U8, tag="zts", name="zt_scales", bufs=2, align_bytes=64)
+            zcs[i] = sb.tile([P, HALVES * P], U32, tag="ztc", name="zt_codes", bufs=2, align_bytes=64)
+            zss[i] = sb.tile([P, HALVES * P], U8, tag="zts", name="zt_scales", bufs=2, align_bytes=64)
             nc.vector.quantize_mx(
                 out=zcs[i][:].bitcast(FP8X4),
                 scales=zss[i][:],
@@ -200,8 +226,8 @@ def tile_reglu_down_two_reads_s8_kernel(
             )
 
         def project(i):
-            ybanks[i] = psum.tile([P, N], F32, tag="m", name="y_acc", bufs=2)
-            for h in range(D_PASSES):
+            ybanks[i] = psum.tile([P, N], F32, tag="mixed", name="y_acc", bufs=2)
+            for h in range(HALVES):
                 toks = slice(h * P, (h + 1) * P)
                 nc.tensor.matmul_mx(
                     out=ybanks[i][:],
@@ -210,47 +236,48 @@ def tile_reglu_down_two_reads_s8_kernel(
                     rhs=head_sb[:, h, :].bitcast(FP4X4),
                     rhs_scale=head_sc[:, h, :],
                     start=(h == 0),
-                    stop=(h == D_PASSES - 1),
+                    stop=(h == HALVES - 1),
                 )
 
         def store_y(i):
-            y = sb.tile([P, N], F32, tag="y", name="y_sb", bufs=3, align_bytes=64)
-            nc.scalar.copy(out=y[:], in_=ybanks[i][:])
-            nc.sync.dma_start(out=y_v[i // PACK][:, i % PACK, :], in_=y[:])
+            y_sb = sb.tile([P, N], F32, tag="y", name="y_sb", bufs=3, align_bytes=64)
+            nc.scalar.copy(out=y_sb[:], in_=ybanks[i][:])
+            nc.sync.dma_start(out=y_v[i // PACK][:, i % PACK, :], in_=y_sb[:])
 
-        def group_z(engine, G, c, d0, d1):
-            if (G, c) not in zis:
-                zis[G, c] = sb.tile([P, CHUNK, PACK], BF16, tag="zi", name="z_grouped", bufs=4, align_bytes=64)
-            dst = zis[G, c][:, d0:d1, :].rearrange("p (c i) t -> p c t i", i=RUN)
-            src = zs[G][:, :, c * CHUNK + d0 : c * CHUNK + d1].rearrange("p t (c i) -> p c t i", i=RUN)
-            if engine == "v":
-                nc.vector.tensor_copy(out=dst, in_=src)
-            else:
-                nc.scalar.copy(out=dst, in_=src)
 
-        def quant_z(G, c):
-            cols = slice(c * CHUNK, (c + 1) * CHUNK)
+        def group_z(copy, G, c, cols=slice(0, CHUNK)):
+            h, c0 = divmod(c * CHUNK, HALF)
+            if (G, h) not in zis:
+                zis[G, h] = sb.tile([P, HALF, PACK], BF16, tag="zi", name="z_grouped", bufs=2, align_bytes=64)
+            copy(
+                out=zis[G, h][:, c0 + cols.start : c0 + cols.stop, :].rearrange("p (c i) t -> p c t i", i=RUN),
+                in_=zs[G][:, :, c * CHUNK + cols.start : c * CHUNK + cols.stop].rearrange(
+                    "p t (c i) -> p c t i", i=RUN
+                ),
+            )
+
+        def quant_z(G, h):
+            cols = slice(h * HALF, (h + 1) * HALF)
             nc.vector.quantize_mx(
                 out=z_codes[:, G, cols].bitcast(FP8X4),
                 scales=z_scales[:, G, cols],
-                in_=zis[G, c][:].rearrange("p d t -> p (d t)"),
+                in_=zis[G, h][:].rearrange("p d t -> p (d t)"),
             )
 
-        def scale_pool(G, a):
-            toks = slice(G * K_PASS, (G + 1) * K_PASS)
+        def scale_pool(a):
             nc.vector.tensor_tensor(
-                out=pool_bf[:, a, toks], in0=code_bytes[:, a, toks].bitcast(FP8), in1=scale_row[:, toks], op=MULT
+                out=pool_bf[:, a, :], in0=code_bytes[:, a, :].bitcast(FP8), in1=scale_row[:], op=MULT
             )
 
         def turn_pool(G, tag):
-            pbanks[G] = psum.tile([P, R // P, 2, P], F32, tag=tag, name="pool_turned", bufs=2)
-            for a in range(R // P):
+            pbanks[G] = psum.tile([P, SLOT_TILES, 2, P], F32, tag=tag, name="pool_turned", bufs=2)
+            for a in range(SLOT_TILES):
                 words = pool_bf[:, a, G * K_PASS : (G + 1) * K_PASS].bitcast(F32)
                 for u in range(2):
                     nc.tensor.transpose(pbanks[G][:, a, u, :], words[:, u : K_PASS // 2 : 2], ident[:])
 
         def empty_pool(G):
-            pts[G] = sb.tile([P, R // P, P, 2], F32, tag="zt", name="pool_grouped", bufs=2, align_bytes=64)
+            pts[G] = sb.tile([P, SLOT_TILES, P, 2], F32, tag="zt", name="pool_grouped", bufs=2, align_bytes=64)
             nc.scalar.copy(out=pts[G][:], in_=pbanks[G][:].rearrange("p a u r -> p a r u"))
 
         def quant_pool(G):
@@ -261,12 +288,11 @@ def tile_reglu_down_two_reads_s8_kernel(
             )
 
         def gather(h, groups):
-            for a in range(R // P):
+            cols = slice(h * HALF, (h + 1) * HALF)
+            for a in range(SLOT_TILES):
                 if (a, h) not in cbanks:
-                    cbanks[a, h] = psum.tile(
-                        [P, HALF], F32, tag=("th", "acc")[h], name="c_acc", bufs=(2, 4)[h]
-                    )
-                cols = slice(h * HALF, (h + 1) * HALF)
+                    tag, bufs = (("turned", 2), ("acc", 4))[h]
+                    cbanks[a, h] = psum.tile([P, HALF], F32, tag=tag, name="c_acc", bufs=bufs)
                 slots = slice(a * P, (a + 1) * P)
                 for G in groups:
                     nc.tensor.matmul_mx(
@@ -279,173 +305,168 @@ def tile_reglu_down_two_reads_s8_kernel(
                         stop=(G == GROUPS - 1),
                     )
 
-        def store_c(engine, a, h):
+        def store_c(copy, a, h):
             c_sb = sb.tile([P, HALF], F32, tag="c", name="c_sb", bufs=4, align_bytes=64)
-            dst = c_sb[:].rearrange("p (q u e) -> p q u e", u=2, e=2)
-            src = cbanks[a, h][:].rearrange("p (u q e) -> p q u e", u=2, e=2)
-            if engine == "v":
-                nc.vector.tensor_copy(out=dst, in_=src)
-            else:
-                nc.scalar.copy(out=dst, in_=src)
+            copy(
+                out=c_sb[:].rearrange("p (q u e) -> p q u e", u=2, e=2),
+                in_=cbanks[a, h][:].rearrange("p (u q e) -> p q u e", u=2, e=2),
+            )
             nc.sync.dma_start(out=out_c[a * P : (a + 1) * P, h * HALF : (h + 1) * HALF], in_=c_sb[:])
 
         with tc.manual_schedule():
-            nc.vector.memset(head_sc[:].rearrange("p g n -> p (g n)").bitcast(I32), 0)
-            nc.vector.memset(warm[:], 0.0)
-            nc.scalar.copy(out=warm[:, 0:1], in_=warm[:, 1:2])
-            make_identity(nc, ident[:])
-
-            load_gate(0)
             load_w(0, 0)
-            load_up(0)
             load_w(1, 0)
+            load_gate(0, LEFT)
+            load_up(0, RIGHT)
+            load_gate(0, RIGHT)
             load_w(2, 0)
+            load_up(0, LEFT)
             load_w(3, 0)
-            load_gate(1)
-            load_up(1)
-            load_resid(0)
             load_w(0, 1)
+            load_gate(1)
             load_w(1, 1)
+            load_up(1)
             load_w(2, 1)
             load_w(3, 1)
+            load_resid(0)
             load_gate(2)
-            load_up(2)
-            load_resid(1)
-            for q in range(4):
-                rows = slice(32 * q, 32 * q + 4)
-                nc.sync.dma_start(
-                    out=head_sc[rows, :, :].bitcast(I32),
-                    in_=head_scales[:, 4 * q : 4 * q + 4, :].rearrange("g q n -> q g n").bitcast(I32),
-                )
-            nc.sync.dma_start(out=head_sb[:], in_=head_words.rearrange("g p b -> p g b"))
             load_gate(3)
+            load_resid(1)
+            load_up(2)
+            load_head()
             load_up(3)
-            load_resid(2)
+            nc.vector.memset(head_sc[:].rearrange("p g n -> p (g n)").bitcast(I32), 0)
+            make_identity(nc, ident[:])
 
-            relu(0)
-            group_w_split(0, 0)
-            product(0)
-            turn_h(0)
+            group_w(0, 0)
+            group_w(1, 0)
+            relu_v(0, LEFT)
             quant_w(0, 0)
-            group_w_split(1, 0)
+            relu_v(0, RIGHT)
+            quant_w(1, 0)
+            product(0, RIGHT)
+            group_w(2, 0)
+            product(0, LEFT)
+            turn_h(0)
+            quant_w(2, 0)
+            group_w(3, 0)
+            group_w(0, 1)
+            relu_v(1, ALL)
+            quant_w(3, 0)
+            quant_w(0, 1)
+            group_w(1, 1)
             empty_h(0, 0)
             empty_h(0, 1)
-            group_w_split(2, 0)
-            quant_w(1, 0)
-            quant_h(0)
-            group_w_split(3, 0)
-            quant_w(2, 0)
-            relu(1)
-            quant_w(3, 0)
-            down(0, 0)
             product(1)
             turn_h(1)
-            group_w_split(0, 1)
-            empty_h(1, 0)
-            empty_h(1, 1)
-            group_w_split(1, 1)
-            quant_w(0, 1)
-            add_resid(0, 0)
-            quant_h(1)
-            group_w_split(2, 1)
-            down(1, 0)
-            quant_w(1, 1)
-            group_w_split(3, 1)
-            quant_w(2, 1)
-            relu(2)
-            quant_w(3, 1)
-            down(0, 1)
-            down(1, 1)
-            product(2)
-            add_resid(1, 0)
-            add_resid(0, 1)
+            group_w(2, 1)
+            quant_h(0)
             load_gate(4)
+            load_head_scales()
+            load_resid(2)
             load_up(4)
-            relu(3)
-            add_resid(1, 1)
+            empty_h(1, 0)
+            down(0, 0)
+            quant_w(2, 1)
+            empty_h(1, 1)
+            quant_w(1, 1)
+            quant_h(1)
+            group_w(3, 1)
+            relu_v(2, ALL)
+            relu_s(3, ALL)
             load_gate(5)
-            load_up(5)
             load_gate(6)
-            load_up(6)
+            load_up(5)
+            quant_w(3, 1)
+            add_resid(0, 0)
+            product(2)
             load_gate(7)
+            down(1, 0)
+            down(0, 1)
+            add_resid(0, 1)
+            load_up(6)
+            down(1, 1)
+            add_resid(1, 0)
+            add_resid(1, 1)
 
-            for s in range(1, TILES):
-                if s + 1 < TILES:
-                    turn_h(s + 1)
-                if s == TILES - 1:
-                    turn_pool(0, "th")
-                    turn_pool(1, "th")
-                turn_z(s - 1)
-                if s >= 2:
-                    store_y(s - 2)
+            for s in range(1, TILES - 1):
                 product(s + 2)
+                if s == 3:
+                    store_y(0)
+                if s == TILES - 2:
+                    scale_pool(0)
+                turn_h(s + 1)
+                turn_z(s - 1)
                 load_resid(s + 2)
-                load_up(s + 6)
-                relu(s + 3)
-                load_gate(s + 7)
-                if s == 4:
-                    nc.sync.dma_start(out=code_bytes[:], in_=pool_bytes.rearrange("(a p) m -> p a m", p=P))
-                    nc.sync.dma_start(out=scale_row[:], in_=pool_scale.rearrange("o k -> (o k)").partition_broadcast(P))
-                if s + 1 < TILES:
-                    empty_h(s + 1, 0)
-                else:
-                    empty_pool(0)
+                if s in (6, 8, 10):
+                    quant_z(*divmod((s - 6) // 2, HALVES))
+                empty_h(s + 1, 0)
                 empty_z(s - 1)
-                if s + 1 < TILES:
-                    empty_h(s + 1, 1)
-                else:
-                    empty_pool(1)
+                empty_h(s + 1, 1)
+                if s >= 3:
+                    store_y(s - 2)
+                if s == 2:
+                    project(0)
+                relu_v(s + 3, RELU_VECTOR)
                 quant_zt(s - 1)
-                if s + 1 < TILES:
-                    quant_h(s + 1)
-                if s >= 5:
-                    quant_z((s - 5) // CHUNKS, (s - 5) % CHUNKS)
-                if s == 9:
-                    scale_pool(0, 0)
-                if s == 10:
-                    scale_pool(0, 1)
-                    scale_pool(1, 0)
-                    scale_pool(1, 1)
-                if s == 11:
-                    quant_pool(0)
-                    quant_pool(1)
-                    scale_pool(2, 0)
-                    scale_pool(2, 1)
                 if s >= 2:
                     down(s, 0)
+                relu_s(s + 3, RELU_SCALAR)
+                if s >= 2:
                     down(s, 1)
+                if s == 4:
+                    load_pool()
+                if s >= 2:
+                    project(s - 1)
                     add_resid(s, 0)
-                    add_resid(s, 1)
+                quant_h(s + 1)
+                load_gate(s + 7)
+                load_up(s + 6)
                 if s >= 4:
-                    group_z("s", (s - 4) // CHUNKS, (s - 4) % CHUNKS, 0, CHUNK)
-                project(s - 1)
+                    group_z(nc.scalar.copy, *divmod(s - 4, PACK))
+                if s >= 2:
+                    add_resid(s, 1)
 
-            last = TILES - 1
-            G = GROUPS - 1
-            group_z("s", G, 0, 0, CHUNK)
-            quant_z(G - 1, CHUNKS - 1)
-            group_z("v", G, 1, 0, CHUNK)
-            gather(0, range(G))
+            last, G = TILES - 1, GROUPS - 1
+            group_z(nc.scalar.copy, G - 1, 3)
+            scale_pool(1)
+            down(last, 0)
+            add_resid(last, 0)
+            turn_z(last - 1)
+            empty_z(last - 1)
+            turn_pool(0, "turned")
+            turn_pool(1, "turned")
+            empty_pool(0)
+            quant_z(G - 1, 1)
+            quant_zt(last - 1)
+            down(last, 1)
+            quant_pool(0)
+            store_y(last - 2)
+            project(last - 1)
+            group_z(nc.vector.tensor_copy, G, 1)
+            add_resid(last, 1)
+            empty_pool(1)
+            quant_pool(1)
+            group_z(nc.scalar.copy, G, 0)
+            group_z(nc.vector.tensor_copy, G, 2)
             turn_z(last)
-            turn_pool(2, "m")
-            gather(1, range(G))
-            store_y(last - 1)
             empty_z(last)
-            group_z("v", G, 2, 0, CHUNK)
-            quant_z(G, 0)
-            quant_z(G, 1)
+            turn_pool(2, "mixed")
             empty_pool(2)
-            group_z("s", G, 3, 0, CHUNK // 2)
+            group_z(nc.scalar.copy, G, 3, slice(0, CHUNK // 2))
+            quant_z(G, 0)
+            gather(0, range(G))
             quant_zt(last)
-            group_z("v", G, 3, CHUNK // 2, CHUNK)
-            quant_pool(2)
-            quant_z(G, 2)
             project(last)
-            quant_z(G, 3)
+            quant_pool(2)
             gather(0, range(G, GROUPS))
-            gather(1, range(G, GROUPS))
+            store_y(last - 1)
             store_y(last)
-            store_c("v", 0, 0)
-            store_c("s", 1, 0)
-            store_c("v", 0, 1)
-            store_c("s", 1, 1)
+            gather(1, range(G))
+            group_z(nc.vector.tensor_copy, G, 3, slice(CHUNK // 2, CHUNK))
+            quant_z(G, 1)
+            gather(1, range(G, GROUPS))
+            store_c(nc.vector.tensor_copy, 0, 0)
+            store_c(nc.scalar.copy, 1, 0)
+            store_c(nc.vector.tensor_copy, 0, 1)
+            store_c(nc.scalar.copy, 1, 1)

from contextlib import ExitStack

import concourse.mybir as mybir
from concourse.masks import make_identity

M, F, D, N, R = 1536, 2048, 1024, 512, 256
FLOPS = 2 * M * F * D + 2 * M * D * N + 2 * R * M * D

F32 = mybir.dt.float32
BF16 = mybir.dt.bfloat16
I32 = mybir.dt.int32
U32 = mybir.dt.uint32
U8 = mybir.dt.uint8
FP8 = mybir.dt.float8_e4m3fn
FP8X4 = mybir.dt.float8_e4m3fn_x4
FP4X4 = mybir.dt.float4_e2m1fn_x4
ADD = mybir.AluOpType.add
MULT = mybir.AluOpType.mult
RELU = mybir.ActivationFunctionType.Relu

P = 128
PACK = 4
K_PASS = P * PACK
TILES = M // P
GROUPS = M // K_PASS
F_PASSES = F // K_PASS
HALF = 512
HALVES = D // HALF
CHUNK = HALF // 2
SLOT_TILES = R // P

W_SPLIT = HALF // 2
ALL = slice(0, F)
LEFT, RIGHT = slice(0, F // 2), slice(F // 2, F)
RELU_VECTOR, RELU_SCALAR = slice(0, 7 * F // 8), slice(7 * F // 8, F)
RUN = 4


def tile_reglu_down_two_reads_s8_kernel(
    tc, gate, up, w_down, resid, head_words, head_scales, pool_bytes, pool_scale, out_y, out_c
):
    nc = tc.nc

    gate_v = gate.rearrange("(g p t) f -> g p t f", p=P, t=PACK)
    up_v = up.rearrange("(g p t) f -> g p t f", p=P, t=PACK)
    resid_v = resid.rearrange("(g p t) d -> g p t d", p=P, t=PACK)
    y_v = out_y.rearrange("(g p t) n -> g p t n", p=P, t=PACK)
    w_v = w_down.rearrange("(g p j) d -> g p j d", p=P, j=PACK)

    with ExitStack() as ctx:
        keep = ctx.enter_context(tc.tile_pool(name="keep", bufs=1))
        sb = ctx.enter_context(tc.tile_pool(name="sb", bufs=2))
        psum = ctx.enter_context(tc.psum_pool(name="psum", bufs=2))

        w_codes = keep.tile([P, F_PASSES, D], U32, name="w_codes", align_bytes=64)
        w_scales = keep.tile([P, F_PASSES, D], U8, name="w_scales", align_bytes=64)
        z_codes = keep.tile([P, GROUPS, D], U32, name="z_codes", align_bytes=64)
        z_scales = keep.tile([P, GROUPS, D], U8, name="z_scales", align_bytes=64)
        pool_codes = keep.tile([P, GROUPS, R], U32, name="pool_codes", align_bytes=64)
        pool_scales = keep.tile([P, GROUPS, R], U8, name="pool_scales", align_bytes=64)
        head_sb = keep.tile([P, HALVES, 2 * N], U8, name="head_sb", align_bytes=64)
        head_sc = keep.tile([P, HALVES, N], U8, name="head_sc", align_bytes=64)
        code_bytes = keep.tile([P, SLOT_TILES, M], U8, name="code_bytes", align_bytes=64)
        scale_row = keep.tile([P, M], F32, name="scale_row", align_bytes=64)
        pool_bf = keep.tile([P, SLOT_TILES, M], BF16, name="pool_bf", align_bytes=64)
        ident = keep.tile([P, P], F32, name="ident", align_bytes=64)

        gates, ups, resids, relus, hs, hbanks, hts, hcs, hss = {}, {}, {}, {}, {}, {}, {}, {}, {}
        accs, zs, zbanks, zts, zcs, zss, ybanks = {}, {}, {}, {}, {}, {}, {}
        wraws, wgs, zis, pbanks, pts, cbanks = {}, {}, {}, {}, {}, {}


        def load_gate(i, cols=ALL):
            if i < TILES:
                if i not in gates:
                    gates[i] = sb.tile([P, F], BF16, tag="gate", name="gate_sb", bufs=4, align_bytes=64)
                nc.sync.dma_start(out=gates[i][:, cols], in_=gate_v[i // PACK][:, i % PACK, cols])

        def load_up(i, cols=ALL):
            if i < TILES:
                if i not in ups:
                    ups[i] = sb.tile([P, F], BF16, tag="up", name="up_sb", bufs=4, align_bytes=64)
                nc.sync.dma_start(out=ups[i][:, cols], in_=up_v[i // PACK][:, i % PACK, cols])

        def load_resid(i):
            if i < TILES:
                resids[i] = sb.tile([P, D], BF16, tag="resid", name="resid_sb", bufs=4, align_bytes=64)
                nc.sync.dma_start(out=resids[i][:], in_=resid_v[i // PACK][:, i % PACK, :])

        def load_w(g, h):
            wraws[g, h] = sb.tile([P, PACK, HALF], BF16, tag="wraw", name="w_raw", bufs=8, align_bytes=64)
            nc.sync.dma_start(out=wraws[g, h][:], in_=w_v[g][:, :, h * HALF : (h + 1) * HALF])

        def load_head():
            nc.sync.dma_start(out=head_sb[:], in_=head_words.rearrange("g p b -> p g b"))

        def load_head_scales():
            for q in range(PACK):
                rows = slice(32 * q, 32 * q + 4)
                nc.sync.dma_start(
                    out=head_sc[rows, :, :].bitcast(I32),
                    in_=head_scales[:, 4 * q : 4 * q + 4, :].rearrange("g q n -> q g n").bitcast(I32),
                )

        def load_pool():
            nc.sync.dma_start(out=scale_row[:], in_=pool_scale.rearrange("o k -> (o k)").partition_broadcast(P))
            nc.sync.dma_start(out=code_bytes[:], in_=pool_bytes.rearrange("(a p) m -> p a m", p=P))


        def group_w(g, h):
            wgs[g, h] = sb.tile([P, HALF, PACK], BF16, tag="wg", name="w_grouped", bufs=3, align_bytes=64)
            for copy, cols in ((nc.scalar.copy, slice(0, W_SPLIT)), (nc.vector.tensor_copy, slice(W_SPLIT, HALF))):
                copy(
                    out=wgs[g, h][:, cols, :].rearrange("p (c i) j -> p c j i", i=RUN),
                    in_=wraws[g, h][:, :, cols].rearrange("p j (c i) -> p c j i", i=RUN),
                )

        def quant_w(g, h):
            cols = slice(h * HALF, (h + 1) * HALF)
            nc.vector.quantize_mx(
                out=w_codes[:, g, cols].bitcast(FP8X4),
                scales=w_scales[:, g, cols],
                in_=wgs[g, h][:].rearrange("p w j -> p (w j)"),
            )


        def relu_tile(i):
            if i not in relus:
                relus[i] = sb.tile([P, F], BF16, tag="relu", name="relu_sb", bufs=2, align_bytes=64)
            return relus[i]

        def relu_v(i, cols):
            if i < TILES:
                nc.vector.tensor_scalar_max(relu_tile(i)[:, cols], gates[i][:, cols], 0.0)

        def relu_s(i, cols):
            if i < TILES:
                nc.scalar.activation(relu_tile(i)[:, cols], gates[i][:, cols], func=RELU)

        def product(i, cols=ALL):
            if i < TILES:
                if i not in hs:
                    hs[i] = sb.tile([P, F], BF16, tag="h", name="h_sb", bufs=2, align_bytes=64)
                quads = slice(cols.start // 4, cols.stop // 4)
                nc.vector.tensor_tensor(
                    out=hs[i][:].rearrange("p (u q e) -> p u q e", u=2, e=2)[:, :, quads, :],
                    in0=relus[i][:, cols].rearrange("p (q u e) -> p u q e", u=2, e=2),
                    in1=ups[i][:, cols].rearrange("p (q u e) -> p u q e", u=2, e=2),
                    op=MULT,
                )

        def turn_h(i):
            words = hs[i][:].bitcast(F32)
            for b in range(2):
                hbanks[i, b] = psum.tile([P, 2, 2, P], F32, tag="turned", name="h_turned", bufs=2)
                for gb in range(2):
                    for u in range(2):
                        w0 = u * (F // 4) + (2 * b + gb) * P
                        nc.tensor.transpose(hbanks[i, b][:, gb, u, :], words[:, w0 : w0 + P], ident[:])

        def empty_h(i, b):
            if i not in hts:
                hts[i] = sb.tile([P, F_PASSES, P, 2], F32, tag="ht", name="h_grouped", bufs=2, align_bytes=64)
            nc.scalar.copy(
                out=hts[i][:, 2 * b : 2 * b + 2, :, :], in_=hbanks[i, b][:].rearrange("p g u m -> p g m u")
            )

        def quant_h(i):
            hcs[i] = sb.tile([P, F_PASSES * P], U32, tag="hc", name="h_codes", bufs=2, align_bytes=64)
            hss[i] = sb.tile([P, F_PASSES * P], U8, tag="hs", name="h_scales", bufs=2, align_bytes=64)
            nc.vector.quantize_mx(
                out=hcs[i][:].bitcast(FP8X4),
                scales=hss[i][:],
                in_=hts[i][:].rearrange("p g m u -> p (g m u)").bitcast(BF16),
            )


        def down(i, h):
            accs[i, h] = psum.tile([P, HALF], F32, tag="acc", name="z_acc", bufs=4)
            cols = slice(h * HALF, (h + 1) * HALF)
            for g in range(F_PASSES):
                toks = slice(g * P, (g + 1) * P)
                nc.tensor.matmul_mx(
                    out=accs[i, h][:],
                    lhsT=hcs[i][:, toks].bitcast(FP8X4),
                    lhsT_scale=hss[i][:, toks],
                    rhs=w_codes[:, g, cols].bitcast(FP8X4),
                    rhs_scale=w_scales[:, g, cols],
                    start=(g == 0),
                    stop=(g == F_PASSES - 1),
                )

        def add_resid(i, h):
            G, t = divmod(i, PACK)
            if G not in zs:
                zs[G] = sb.tile([P, PACK, D], BF16, tag="z", name="z_sb", bufs=2, align_bytes=64)
            cols = slice(h * HALF, (h + 1) * HALF)
            nc.vector.tensor_tensor(
                out=zs[G][:, t, cols].rearrange("p (u q e) -> p u q e", u=2, e=2),
                in0=accs[i, h][:].rearrange("p (q u e) -> p u q e", u=2, e=2),
                in1=resids[i][:, cols].rearrange("p (q u e) -> p u q e", u=2, e=2),
                op=ADD,
            )


        def turn_z(i):
            G, t = divmod(i, PACK)
            words = zs[G][:, t, :].bitcast(F32)
            zbanks[i] = psum.tile([P, HALVES, 2, P], F32, tag="mixed", name="z_turned", bufs=2)
            for h in range(HALVES):
                for u in range(2):
                    w0 = h * (HALF // 2) + u * P
                    nc.tensor.transpose(zbanks[i][:, h, u, :], words[:, w0 : w0 + P], ident[:])

        def empty_z(i):
            zts[i] = sb.tile([P, HALVES, P, 2], F32, tag="zt", name="zt_grouped", bufs=2, align_bytes=64)
            nc.scalar.copy(out=zts[i][:], in_=zbanks[i][:].rearrange("p h u m -> p h m u"))

        def quant_zt(i):
            zcs[i] = sb.tile([P, HALVES * P], U32, tag="ztc", name="zt_codes", bufs=2, align_bytes=64)
            zss[i] = sb.tile([P, HALVES * P], U8, tag="zts", name="zt_scales", bufs=2, align_bytes=64)
            nc.vector.quantize_mx(
                out=zcs[i][:].bitcast(FP8X4),
                scales=zss[i][:],
                in_=zts[i][:].rearrange("p h m u -> p (h m u)").bitcast(BF16),
            )

        def project(i):
            ybanks[i] = psum.tile([P, N], F32, tag="mixed", name="y_acc", bufs=2)
            for h in range(HALVES):
                toks = slice(h * P, (h + 1) * P)
                nc.tensor.matmul_mx(
                    out=ybanks[i][:],
                    lhsT=zcs[i][:, toks].bitcast(FP8X4),
                    lhsT_scale=zss[i][:, toks],
                    rhs=head_sb[:, h, :].bitcast(FP4X4),
                    rhs_scale=head_sc[:, h, :],
                    start=(h == 0),
                    stop=(h == HALVES - 1),
                )

        def store_y(i):
            y_sb = sb.tile([P, N], F32, tag="y", name="y_sb", bufs=3, align_bytes=64)
            nc.scalar.copy(out=y_sb[:], in_=ybanks[i][:])
            nc.sync.dma_start(out=y_v[i // PACK][:, i % PACK, :], in_=y_sb[:])


        def group_z(copy, G, c, cols=slice(0, CHUNK)):
            h, c0 = divmod(c * CHUNK, HALF)
            if (G, h) not in zis:
                zis[G, h] = sb.tile([P, HALF, PACK], BF16, tag="zi", name="z_grouped", bufs=2, align_bytes=64)
            copy(
                out=zis[G, h][:, c0 + cols.start : c0 + cols.stop, :].rearrange("p (c i) t -> p c t i", i=RUN),
                in_=zs[G][:, :, c * CHUNK + cols.start : c * CHUNK + cols.stop].rearrange(
                    "p t (c i) -> p c t i", i=RUN
                ),
            )

        def quant_z(G, h):
            cols = slice(h * HALF, (h + 1) * HALF)
            nc.vector.quantize_mx(
                out=z_codes[:, G, cols].bitcast(FP8X4),
                scales=z_scales[:, G, cols],
                in_=zis[G, h][:].rearrange("p d t -> p (d t)"),
            )

        def scale_pool(a):
            nc.vector.tensor_tensor(
                out=pool_bf[:, a, :], in0=code_bytes[:, a, :].bitcast(FP8), in1=scale_row[:], op=MULT
            )

        def turn_pool(G, tag):
            pbanks[G] = psum.tile([P, SLOT_TILES, 2, P], F32, tag=tag, name="pool_turned", bufs=2)
            for a in range(SLOT_TILES):
                words = pool_bf[:, a, G * K_PASS : (G + 1) * K_PASS].bitcast(F32)
                for u in range(2):
                    nc.tensor.transpose(pbanks[G][:, a, u, :], words[:, u : K_PASS // 2 : 2], ident[:])

        def empty_pool(G):
            pts[G] = sb.tile([P, SLOT_TILES, P, 2], F32, tag="zt", name="pool_grouped", bufs=2, align_bytes=64)
            nc.scalar.copy(out=pts[G][:], in_=pbanks[G][:].rearrange("p a u r -> p a r u"))

        def quant_pool(G):
            nc.vector.quantize_mx(
                out=pool_codes[:, G, :].bitcast(FP8X4),
                scales=pool_scales[:, G, :],
                in_=pts[G][:].rearrange("p a r u -> p (a r u)").bitcast(BF16),
            )

        def gather(h, groups):
            cols = slice(h * HALF, (h + 1) * HALF)
            for a in range(SLOT_TILES):
                if (a, h) not in cbanks:
                    tag, bufs = (("turned", 2), ("acc", 4))[h]
                    cbanks[a, h] = psum.tile([P, HALF], F32, tag=tag, name="c_acc", bufs=bufs)
                slots = slice(a * P, (a + 1) * P)
                for G in groups:
                    nc.tensor.matmul_mx(
                        out=cbanks[a, h][:],
                        lhsT=pool_codes[:, G, slots].bitcast(FP8X4),
                        lhsT_scale=pool_scales[:, G, slots],
                        rhs=z_codes[:, G, cols].bitcast(FP8X4),
                        rhs_scale=z_scales[:, G, cols],
                        start=(G == 0),
                        stop=(G == GROUPS - 1),
                    )

        def store_c(copy, a, h):
            c_sb = sb.tile([P, HALF], F32, tag="c", name="c_sb", bufs=4, align_bytes=64)
            copy(
                out=c_sb[:].rearrange("p (q u e) -> p q u e", u=2, e=2),
                in_=cbanks[a, h][:].rearrange("p (u q e) -> p q u e", u=2, e=2),
            )
            nc.sync.dma_start(out=out_c[a * P : (a + 1) * P, h * HALF : (h + 1) * HALF], in_=c_sb[:])

        with tc.manual_schedule():
            load_w(0, 0)
            load_w(1, 0)
            load_gate(0, LEFT)
            load_up(0, RIGHT)
            load_gate(0, RIGHT)
            load_w(2, 0)
            load_up(0, LEFT)
            load_w(3, 0)
            load_w(0, 1)
            load_gate(1)
            load_w(1, 1)
            load_up(1)
            load_w(2, 1)
            load_w(3, 1)
            load_resid(0)
            load_gate(2)
            load_gate(3)
            load_resid(1)
            load_up(2)
            load_head()
            load_up(3)
            nc.vector.memset(head_sc[:].rearrange("p g n -> p (g n)").bitcast(I32), 0)
            make_identity(nc, ident[:])

            group_w(0, 0)
            group_w(1, 0)
            relu_v(0, LEFT)
            quant_w(0, 0)
            relu_v(0, RIGHT)
            quant_w(1, 0)
            product(0, RIGHT)
            group_w(2, 0)
            product(0, LEFT)
            turn_h(0)
            quant_w(2, 0)
            group_w(3, 0)
            group_w(0, 1)
            relu_v(1, ALL)
            quant_w(3, 0)
            quant_w(0, 1)
            group_w(1, 1)
            empty_h(0, 0)
            empty_h(0, 1)
            product(1)
            turn_h(1)
            group_w(2, 1)
            quant_h(0)
            load_gate(4)
            load_head_scales()
            load_resid(2)
            load_up(4)
            empty_h(1, 0)
            down(0, 0)
            quant_w(2, 1)
            empty_h(1, 1)
            quant_w(1, 1)
            quant_h(1)
            group_w(3, 1)
            relu_v(2, ALL)
            relu_s(3, ALL)
            load_gate(5)
            load_gate(6)
            load_up(5)
            quant_w(3, 1)
            add_resid(0, 0)
            product(2)
            load_gate(7)
            down(1, 0)
            down(0, 1)
            add_resid(0, 1)
            load_up(6)
            down(1, 1)
            add_resid(1, 0)
            add_resid(1, 1)

            for s in range(1, TILES - 1):
                product(s + 2)
                if s == 3:
                    store_y(0)
                if s == TILES - 2:
                    scale_pool(0)
                turn_h(s + 1)
                turn_z(s - 1)
                load_resid(s + 2)
                if s in (6, 8, 10):
                    quant_z(*divmod((s - 6) // 2, HALVES))
                empty_h(s + 1, 0)
                empty_z(s - 1)
                empty_h(s + 1, 1)
                if s >= 3:
                    store_y(s - 2)
                if s == 2:
                    project(0)
                relu_v(s + 3, RELU_VECTOR)
                quant_zt(s - 1)
                if s >= 2:
                    down(s, 0)
                relu_s(s + 3, RELU_SCALAR)
                if s >= 2:
                    down(s, 1)
                if s == 4:
                    load_pool()
                if s >= 2:
                    project(s - 1)
                    add_resid(s, 0)
                quant_h(s + 1)
                load_gate(s + 7)
                load_up(s + 6)
                if s >= 4:
                    group_z(nc.scalar.copy, *divmod(s - 4, PACK))
                if s >= 2:
                    add_resid(s, 1)

            last, G = TILES - 1, GROUPS - 1
            group_z(nc.scalar.copy, G - 1, 3)
            scale_pool(1)
            down(last, 0)
            add_resid(last, 0)
            turn_z(last - 1)
            empty_z(last - 1)
            turn_pool(0, "turned")
            turn_pool(1, "turned")
            empty_pool(0)
            quant_z(G - 1, 1)
            quant_zt(last - 1)
            down(last, 1)
            quant_pool(0)
            store_y(last - 2)
            project(last - 1)
            group_z(nc.vector.tensor_copy, G, 1)
            add_resid(last, 1)
            empty_pool(1)
            quant_pool(1)
            group_z(nc.scalar.copy, G, 0)
            group_z(nc.vector.tensor_copy, G, 2)
            turn_z(last)
            empty_z(last)
            turn_pool(2, "mixed")
            empty_pool(2)
            group_z(nc.scalar.copy, G, 3, slice(0, CHUNK // 2))
            quant_z(G, 0)
            gather(0, range(G))
            quant_zt(last)
            project(last)
            quant_pool(2)
            gather(0, range(G, GROUPS))
            store_y(last - 1)
            store_y(last)
            gather(1, range(G))
            group_z(nc.vector.tensor_copy, G, 3, slice(CHUNK // 2, CHUNK))
            quant_z(G, 1)
            gather(1, range(G, GROUPS))
            store_c(nc.vector.tensor_copy, 0, 0)
            store_c(nc.scalar.copy, 1, 0)
            store_c(nc.vector.tensor_copy, 0, 1)
            store_c(nc.scalar.copy, 1, 1)
